import numpy as np
import ml_dtypes


def mxq(x, axis, fmt="e4m3"):
    dtype, down = {"e4m3": (ml_dtypes.float8_e4m3fn, 7), "e5m2": (ml_dtypes.float8_e5m2, 14)}[fmt]
    v = np.moveaxis(np.asarray(x, np.float32).astype(ml_dtypes.bfloat16).astype(np.float64), axis, -1)
    blocks = v.reshape(v.shape[:-1] + (-1, 32))
    amax = np.abs(blocks).max(-1, keepdims=True)
    byte = np.maximum(np.where(amax > 0, np.frexp(amax)[1] - 1 + 127, 0) - down, 1)
    scale = np.exp2(byte - 127.0)
    codes = (blocks / scale).astype(np.float32).astype(dtype).astype(np.float64)
    return np.moveaxis((codes * scale).reshape(v.shape), -1, axis)


WIDE = False


def mx_kscale(k):
    if not WIDE:
        return np.ones(k)
    levels = np.array([10, -10, 5, -5, 0])
    if k % 512:
        return np.exp2(np.random.permutation(np.resize(levels, k // 32))).repeat(32)
    a = np.empty((k // 512, 16))
    for p in range(k // 512):
        a[p, :8] = np.random.permutation(np.resize(levels, 8))
        for g in range(8):
            far = levels[np.abs(levels - a[p, g]) >= 10]
            a[p, g + 8] = far[np.random.randint(len(far))]
    return np.exp2(a.ravel()).repeat(32)


def f64(x):
    return np.asarray(x).astype(np.float64)


def striped(idx):
    return np.tile(idx.reshape(-1, 16).T, (8, 1)).astype(np.uint16)


def unstriped(offs):
    return offs[:16].T.reshape(-1).astype(np.int64)


def striped8(idx):
    return np.concatenate([x.reshape(-1, 16).T for x in idx]).astype(np.uint16)


def runs(offs, k):
    lists = np.stack([offs[16 * r : 16 * r + 16].T.reshape(-1) for r in range(8)]).astype(np.int64)
    return lists[np.arange(k) % 512 // 64]


def pack_weight(w):
    k, n = w.shape
    w = f64(np.asarray(w, np.float32).astype(ml_dtypes.bfloat16)).reshape(k // 32, 32, n)
    amax = np.abs(w).max(1)
    byte = np.clip(np.where(amax > 0, np.frexp(amax)[1] - 1 + 127 - 7, 1), 1, 254)
    scaled = (w * np.exp2(127.0 - byte)[:, None, :]).reshape(k, n).astype(np.float32)
    words = np.ascontiguousarray(scaled.reshape(k // 512, 128, 4, n).transpose(0, 1, 3, 2)).astype(ml_dtypes.float8_e4m3fn).view(np.uint8)
    return words, np.ascontiguousarray(byte.astype(np.uint8).reshape(k // 512, 16, n))


def unpack_weight(words, scales):
    g, p, n, _ = words.shape
    vals = np.ascontiguousarray(words).view(ml_dtypes.float8_e4m3fn).astype(np.float64) * np.repeat(np.exp2(scales.astype(np.float64) - 127.0), 8, axis=1)[..., None]
    return vals.transpose(0, 1, 3, 2).reshape(g * 512, n)


E2M1 = np.array([0.0, 0.5, 1.0, 1.5, 2.0, 3.0, 4.0, 6.0, -0.0, -0.5, -1.0, -1.5, -2.0, -3.0, -4.0, -6.0])


def pack_fp4(w):
    k, n = w.shape
    w = f64(np.asarray(w, np.float32).astype(ml_dtypes.bfloat16)).reshape(k // 32, 32, n)
    amax = np.abs(w).max(1)
    mant, ex = np.frexp(amax / 6.0)
    byte = np.clip(np.where(amax > 0, np.where(mant > 0.5, ex, ex - 1) + 127, 1), 1, 254)
    scaled = (w * np.exp2(127.0 - byte)[:, None, :]).reshape(k, n).astype(np.float32)
    c = np.ascontiguousarray(scaled.reshape(k // 512, 128, 4, n).transpose(0, 1, 3, 2)).astype(ml_dtypes.float4_e2m1fn).view(np.uint8) & 0xF
    words = (c[..., 0::2] | (c[..., 1::2] << 4)).reshape(k // 512, 128, 2 * n)
    return np.ascontiguousarray(words), np.ascontiguousarray(byte.astype(np.uint8).reshape(k // 512, 16, n))


def unpack_fp4(words, scales):
    g, _, n = scales.shape
    words = np.ascontiguousarray(words).reshape(g, 128, n, 2)
    nib = np.empty((g, 128, n, 4), np.uint8)
    nib[..., 0::2] = words & 0xF
    nib[..., 1::2] = words >> 4
    vals = E2M1[nib] * np.repeat(np.exp2(scales.astype(np.float64) - 127.0), 8, axis=1)[..., None]
    return vals.transpose(0, 1, 3, 2).reshape(g * 512, n)


def planes(y):
    n, m = y.shape
    v = y.astype(np.float32).astype(ml_dtypes.bfloat16).astype(np.float64).reshape(n // 32, 32, m)
    top = np.abs(v).max(1)
    byte = np.clip(np.where(top > 0, np.frexp(top)[1] - 1 + 127 - 7, 1), 1, 254)
    codes = (v * np.exp2(127.0 - byte)[:, None, :]).reshape(n, m).astype(np.float32).astype(ml_dtypes.float8_e4m3fn).view(np.uint8)
    words = codes.reshape(n // 512, 128, 4, m).transpose(0, 1, 3, 2)
    return np.ascontiguousarray(words), np.ascontiguousarray(byte.astype(np.uint8).reshape(n // 512, 16, m))


K, T, S, V, H = 512, 2048, 512, 512, 512


def setup_inputs():
    n = np.random.standard_normal
    s = mx_kscale(K)[:, None]
    u = mx_kscale(S)
    packed_xT = pack_weight(n((K, T)) * s)
    packed_w1 = pack_fp4(n((K, H)) / np.sqrt(K) / s)
    packed_w2 = pack_fp4(n((K, H)) / np.sqrt(K) / s)
    packed_w3 = pack_fp4(n((K, H)) / np.sqrt(K) / s)
    return {
        "x_words": packed_xT[0],
        "x_scales": packed_xT[1],
        "w1_words": packed_w1[0],
        "w1_scales": packed_w1[1],
        "w2_words": packed_w2[0],
        "w2_scales": packed_w2[1],
        "w3_words": packed_w3[0],
        "w3_scales": packed_w3[1],
        "ga": (np.random.uniform(0.5, 1.5, (H, 1)) * u[:, None]).astype(np.float32),
        "gb": (np.random.uniform(0.5, 1.5, (H, 1)) / u[:, None]).astype(np.float32),
        "offs": striped(np.random.permutation(T)[:S]),
        "two": striped(np.random.permutation(T)[:S]),
        "n1": striped8(np.stack([np.random.permutation(S) for _ in range(8)])),
        "n2": striped8(np.stack([np.random.permutation(S) for _ in range(8)])),
        "three": striped(np.random.permutation(T)[:V]),
        "n3": striped8(np.stack([np.random.permutation(V) for _ in range(8)])),
        "n4": striped8(np.stack([np.random.permutation(V) for _ in range(8)])),
        "n5": striped8(np.stack([np.random.permutation(V) for _ in range(8)])),
        "n6": striped8(np.stack([np.random.permutation(V) for _ in range(8)])),
    }


def reference(x_words, x_scales, w1_words, w1_scales, w2_words, w2_scales, w3_words, w3_scales, ga, gb, offs, two, n1, n2, three, n3, n4, n5, n6):
    xq = unpack_weight(x_words, x_scales)[:, unstriped(offs)]
    y = unpack_fp4(w1_words, w1_scales).T @ xq
    x_two = unpack_weight(x_words, x_scales)[:, unstriped(two)]
    d = unpack_fp4(w2_words, w2_scales).T @ x_two
    z = f64(ga) * (y * (np.tanh(d[np.arange(H)[:, None], runs(n1, H)] - (d[np.arange(H)[:, None], runs(n2, H)]))))
    x_three = unpack_weight(x_words, x_scales)[:, unstriped(three)]
    b = unpack_fp4(w3_words, w3_scales).T @ x_three
    z2 = f64(gb) * ((b[np.arange(H)[:, None], runs(n3, H)]) / (np.abs(b) + np.abs(b[np.arange(H)[:, None], runs(n4, H)]) + 0.5))
    s = 0.0625 * ((mxq(z, 0, "e4m3").T @ mxq(z2, 0, "e4m3")))
    st = s + s[np.arange(S)[:, None], runs(n5, S)]
    out_0 = st * (np.tanh(st[np.arange(S)[:, None], runs(n6, S)]))
    return (out_0,) + planes(out_0)

@@ -1,0 +1,267 @@
+from contextlib import ExitStack
+
+import concourse.mybir as mybir
+from concourse.masks import make_identity
+
+F32 = mybir.dt.float32
+BF16 = mybir.dt.bfloat16
+I32 = mybir.dt.int32
+U32 = mybir.dt.uint32
+U16 = mybir.dt.uint16
+U8 = mybir.dt.uint8
+FP8X4 = mybir.dt.float8_e4m3fn_x4
+FP4X4 = mybir.dt.float4_e2m1fn_x4
+ALU = mybir.AluOpType
+ACT = mybir.ActivationFunctionType
+
+P = 128
+T = 2048
+N = 512
+J = 4
+
+FLOPS = 4 * 2 * 512 * 512 * 512
+
+
+def tile_picked_twkjointbnorm2hopp_none_po_kernel(
+    tc, x_words, x_scales, w1_words, w1_scales, w2_words, w2_scales, w3_words, w3_scales,
+    ga, gb, offs, two, n1, n2, three, n3, n4, n5, n6, out_0, out_1, out_2,
+):
+    nc = tc.nc
+    with ExitStack() as ctx:
+        keep = ctx.enter_context(tc.tile_pool(name="keep", bufs=1))
+        psum = ctx.enter_context(tc.psum_pool(name="psum", bufs=1))
+
+        def sb(name, shape, dtype, tag=None):
+            return keep.tile(shape, dtype, name=name, tag=tag or name, align_bytes=64)
+
+        def bank(k, name):
+            return psum.tile([P, N], F32, name=name, tag="bank%d" % k)
+
+        def load_list(name, src):
+            tile = sb(name, [P, N // 16], U16)
+            nc.sync.dma_start(tile[:], src)
+            return tile
+
+        def load_scale_rows(queue, tile, src):
+            for q in range(4):
+                queue.dma_start(tile[32 * q : 32 * q + 4, :].bitcast(I32), src[0, 4 * q : 4 * q + 4, :].bitcast(I32))
+
+        xs = sb("xs", [P, T], U8)
+        nc.vector.memset(xs[:].bitcast(I32), 0)
+        ws_raw = [sb("ws_raw%d" % a, [P, N], U8) for a in range(3)]
+        for a in (2, 1, 0):
+            nc.vector.memset(ws_raw[a][:].bitcast(I32), 0)
+        win_abs = [sb("win_abs%d" % j, [P, 2 * N], F32) for j in range(J)]
+        win_num = [sb("win_num%d" % j, [P, 2 * N], F32) for j in range(J)]
+        win_d = [sb("win_d%d" % j, [P, 2 * N], F32) for j in range(J)]
+        for j in range(J):
+            nc.vector.memset(win_abs[j][:, N:], 0.0)
+
+        half = sb("half", [P, 1], F32)
+        nc.gpsimd.memset(half[:], 0.5)
+        warm = sb("warm", [P, 1], F32)
+        nc.scalar.activation(warm[:], half[:], ACT.Ln)
+        gain_rows = sb("gain_rows", [P, P], F32)
+        nc.gpsimd.memset(gain_rows[:], 0.0)
+        for r, gain in enumerate((ga, gb)):
+            nc.gpsimd.dma_start(
+                gain_rows[J * r : J * r + J, :].rearrange("j (g i) -> j g i", i=8),
+                gain.rearrange("(g j i) o -> j g (i o)", j=J, i=8),
+            )
+        ident = sb("ident", [P, P], F32)
+        make_identity(nc, ident[:])
+
+        l_three = load_list("l_three", three)
+        load_scale_rows(nc.sync, xs, x_scales)
+        l_two = load_list("l_two", two)
+        xw = sb("xw", [P, T], I32)
+        nc.sync.dma_start(xw[:], x_words[0].rearrange("p n t -> p (n t)").bitcast(I32))
+        ww_raw = [sb("ww_raw%d" % a, [P, 2 * N], U8) for a in range(3)]
+        w_words = (w1_words, w2_words, w3_words)
+        w_scales = (w1_scales, w2_scales, w3_scales)
+
+        def load_weight(a):
+            nc.sync.dma_start(ww_raw[a][:].bitcast(I32), w_words[a][0].bitcast(I32))
+            load_scale_rows(nc.sync, ws_raw[a], w_scales[a])
+
+        load_weight(2)
+        l_offs = load_list("l_offs", offs)
+        load_weight(1)
+        l_n4 = load_list("l_n4", n4)
+        load_weight(0)
+        l_n2 = load_list("l_n2", n2)
+        l_n1 = load_list("l_n1", n1)
+        l_n3 = load_list("l_n3", n3)
+        l_n5 = load_list("l_n5", n5)
+        l_n6 = load_list("l_n6", n6)
+
+        gain_ps = bank(7, "gain_ps")
+        nc.tensor.transpose(gain_ps[:, :P], gain_rows[:], ident[:])
+        gains = sb("gains", [P, 2 * J], F32)
+        nc.scalar.copy(gains[:], gain_ps[:, : 2 * J])
+
+        lists = (l_offs, l_two, l_three)
+        xs_g = [sb("xs_g%d" % a, [P, N], U8) for a in range(3)]
+        ww = [sb("ww%d" % a, [P, 2 * N], U8) for a in range(3)]
+        ws = [sb("ws%d" % a, [P, N], U8) for a in range(3)]
+
+        def pick_scales(a):
+            nc.vector.tensor_copy(xs_g[a][:], xs[:].indirect(lists[a][:]))
+
+        pick_scales(2)
+        pick_scales(1)
+
+        def project(a, first_bank):
+            nc.vector.tensor_copy(
+                ww[a][:].bitcast(I32).rearrange("p (j g w) -> p j g w", j=J, w=4),
+                ww_raw[a][:].bitcast(I32).rearrange("p (g j w) -> p j g w", j=J, w=4),
+            )
+            nc.vector.tensor_copy(
+                ws[a][:].bitcast(I32).rearrange("p (j g w) -> p j g w", j=J, w=2),
+                ws_raw[a][:].bitcast(I32).rearrange("p (g j w) -> p j g w", j=J, w=2),
+            )
+            xw_g = sb("xw_g%d" % a, [P, N], I32, tag="ws_raw%d" % (a + 1))
+            nc.vector.tensor_copy(xw_g[:].bitcast(U32), xw[:].bitcast(U32).indirect(lists[a][:]))
+            banks = []
+            for j in range(J):
+                acc = bank(first_bank + j, "proj%d_%d" % (a, j))
+                nc.tensor.matmul_mx(
+                    acc[:],
+                    lhsT=ww[a][:, 2 * P * j : 2 * P * (j + 1)].bitcast(FP4X4),
+                    lhsT_scale=ws[a][:, P * j : P * (j + 1)],
+                    rhs=xw_g[:].bitcast(FP8X4),
+                    rhs_scale=xs_g[a][:],
+                    start=True,
+                    stop=True,
+                )
+                banks.append(acc)
+            return banks
+
+        b_ps = project(2, 0)
+        for j in range(J):
+            nc.scalar.activation(win_abs[j][:, :N], b_ps[j][:], ACT.Abs)
+            if j == 0:
+                nc.scalar.activation(win_num[j][:, N:], b_ps[j][:], ACT.Abs)
+            else:
+                nc.sync.dma_start(win_num[j][:, N:], win_abs[j][:, :N])
+        d_ps = project(1, 4)
+        for j in range(J):
+            nc.scalar.copy(win_d[j][:, :N], d_ps[j][:])
+        for j in range(J):
+            nc.scalar.activation(win_num[j][:, :N], b_ps[j][:], ACT.Copy, scale=gains[:, J + j : J + j + 1])
+        pick_scales(0)
+        y_ps = project(0, 0)
+
+        for j in range(J):
+            nc.vector.tensor_tensor(win_d[j][:, N:], win_abs[j][:].indirect(l_n4[:]), win_num[j][:, N:], ALU.add)
+        lnden = sb("lnden", [P, J, N], F32)
+        for j in range(J):
+            nc.scalar.activation(lnden[:, j, :], win_d[j][:, N:], ACT.Ln, bias=half[:])
+        rec = sb("rec", [P, J, N], F32)
+        for j in range(J):
+            nc.scalar.activation(rec[:, j, :], lnden[:, j, :], ACT.Exp, scale=-1.0)
+
+        d2 = sb("d2", [P, J, N], F32)
+        for j in range(J):
+            nc.vector.tensor_copy(d2[:, j, :], win_d[j][:].indirect(l_n2[:]))
+        th = sb("th", [P, J, N], F32)
+        yg = lnden
+        z2f = sb("z2f", [P, J, N], F32)
+
+        def difference(j):
+            diff = rec[:, j, :]
+            nc.vector.tensor_tensor(diff, win_d[j][:].indirect(l_n1[:]), d2[:, j, :], ALU.subtract)
+            nc.scalar.activation(
+                th[:, j, :].rearrange("p (u m) -> p m u", u=J),
+                diff.rearrange("p (m u) -> p m u", u=J),
+                ACT.Tanh,
+            )
+
+        for j in range(J):
+            nc.vector.tensor_tensor(z2f[:, j, :], win_num[j][:].indirect(l_n3[:]), rec[:, j, :], ALU.mult)
+        for j in range(J):
+            nc.scalar.activation(
+                yg[:, j, :].rearrange("p (u m) -> p u m", u=J),
+                y_ps[j][:].rearrange("p (m u) -> p u m", u=J),
+                ACT.Copy,
+                scale=gains[:, j : j + 1],
+            )
+        z2b = sb("z2b", [P, J * N], BF16)
+        nc.scalar.copy(
+            z2b[:].rearrange("p (c i j) -> p c j i", i=4, j=J),
+            z2f[:].rearrange("p j (c i) -> p c j i", i=4),
+        )
+        for j in range(J):
+            difference(j)
+        z2w = sb("z2w", [P, N], U32)
+        z2s = sb("z2s", [P, N], U8)
+        nc.vector.quantize_mx(out=z2w[:].bitcast(FP8X4), scales=z2s[:], in_=z2b[:])
+
+        zb = [sb("zb%d" % u, [P, J * P], BF16) for u in range(J)]
+        zw = [sb("zw%d" % u, [P, P], U32) for u in range(J)]
+        zs = [sb("zs%d" % u, [P, P], U8) for u in range(J)]
+
+        def make_z(u):
+            cols = slice(P * u, P * (u + 1))
+            nc.vector.tensor_tensor(
+                zb[u][:].rearrange("p (c i j) -> p c j i", i=4, j=J),
+                yg[:, :, cols].rearrange("p j (c i) -> p c j i", i=4),
+                th[:, :, cols].rearrange("p j (c i) -> p c j i", i=4),
+                ALU.mult,
+            )
+
+        def scores(u):
+            nc.vector.quantize_mx(out=zw[u][:].bitcast(FP8X4), scales=zs[u][:], in_=zb[u][:])
+            acc = bank(4 + u, "s_ps%d" % u)
+            nc.tensor.matmul_mx(
+                acc[:],
+                lhsT=zw[u][:].bitcast(FP8X4),
+                lhsT_scale=zs[u][:],
+                rhs=z2w[:].bitcast(FP8X4),
+                rhs_scale=z2s[:],
+                start=True,
+                stop=True,
+            )
+            nc.scalar.activation(win_abs[u][:, :N], acc[:], ACT.Copy, scale=0.0625)
+            nc.scalar.activation(win_num[u][:, N:], acc[:], ACT.Copy, scale=0.0625)
+
+        make_z(0)
+        for u in range(J):
+            if u + 1 < J:
+                make_z(u + 1)
+            scores(u)
+
+        st = sb("st", [P, J, N], F32)
+        for u in range(J):
+            nc.vector.tensor_tensor(st[:, u, :], win_abs[u][:].indirect(l_n5[:]), win_num[u][:, N:], ALU.add)
+            nc.scalar.activation(win_num[u][:, :N], st[:, u, :], ACT.Tanh)
+
+        out_rows = out_0.rearrange("(p u) v -> p u v", u=J)
+        words_out = out_1[0].rearrange("p n t -> p (n t)").bitcast(I32)
+        ow = sb("ow", [P, N], I32)
+        osc = sb("osc", [P, N], U8)
+        chunks = ((0, 256), (256, 384), (384, 512))
+        res = [sb("res%d" % c, [P, J, hi - lo], F32) for c, (lo, hi) in enumerate(chunks)]
+        resb = [sb("resb%d" % c, [P, J * (hi - lo)], BF16) for c, (lo, hi) in enumerate(chunks)]
+
+        def quantise_out(c):
+            lo, hi = chunks[c]
+            nc.vector.quantize_mx(out=ow[:, lo:hi].bitcast(FP8X4), scales=osc[:, lo:hi], in_=resb[c][:])
+            nc.sync.dma_start(words_out[:, lo:hi], ow[:, lo:hi])
+
+        for c, (lo, hi) in enumerate(chunks):
+            for u in range(J):
+                nc.vector.tensor_tensor(
+                    res[c][:, u, :], win_num[u][:].indirect(l_n6[:, lo // 16 : hi // 16]), st[:, u, lo:hi], ALU.mult
+                )
+            nc.sync.dma_start(out_rows[:, :, lo:hi], res[c][:])
+            engine_copy = nc.scalar.copy if c + 1 < len(chunks) else nc.vector.tensor_copy
+            engine_copy(
+                resb[c][:].rearrange("p (c i u) -> p c u i", i=4, u=J),
+                res[c][:].rearrange("p u (c i) -> p c u i", i=4),
+            )
+        for c in range(len(chunks)):
+            quantise_out(c)
+        for q in range(4):
+            queue = nc.scalar if q % 2 else nc.sync
+            queue.dma_start(out_2[0, 4 * q : 4 * q + 4, :].bitcast(I32), osc[32 * q : 32 * q + 4, :].bitcast(I32))

@@ -47,15 +47,13 @@ def tile_picked_twkjointbnorm2hopp_none_po_kernel(
                 queue.dma_start(tile[32 * q : 32 * q + 4, :].bitcast(I32), src[0, 4 * q : 4 * q + 4, :].bitcast(I32))
 
         xs = sb("xs", [P, T], U8)
-        nc.vector.memset(xs[:].bitcast(I32), 0)
+        nc.gpsimd.memset(xs[:].bitcast(I32), 0)
         ws_raw = [sb("ws_raw%d" % a, [P, N], U8) for a in range(3)]
         for a in (2, 1, 0):
             nc.vector.memset(ws_raw[a][:].bitcast(I32), 0)
         win_abs = [sb("win_abs%d" % j, [P, 2 * N], F32) for j in range(J)]
         win_num = [sb("win_num%d" % j, [P, 2 * N], F32) for j in range(J)]
         win_d = [sb("win_d%d" % j, [P, 2 * N], F32) for j in range(J)]
-        for j in range(J):
-            nc.vector.memset(win_abs[j][:, N:], 0.0)
 
         half = sb("half", [P, 1], F32)
         nc.gpsimd.memset(half[:], 0.5)
@@ -120,7 +118,7 @@ def tile_picked_twkjointbnorm2hopp_none_po_kernel(
                 ws[a][:].bitcast(I32).rearrange("p (j g w) -> p j g w", j=J, w=2),
                 ws_raw[a][:].bitcast(I32).rearrange("p (g j w) -> p j g w", j=J, w=2),
             )
-            xw_g = sb("xw_g%d" % a, [P, N], I32, tag="ws_raw%d" % (a + 1))
+            xw_g = sb("xw_g%d" % a, [P, N], I32, tag="ws_raw%d" % a)
             nc.vector.tensor_copy(xw_g[:].bitcast(U32), xw[:].bitcast(U32).indirect(lists[a][:]))
             banks = []
             for j in range(J):
@@ -141,9 +139,9 @@ def tile_picked_twkjointbnorm2hopp_none_po_kernel(
         for j in range(J):
             nc.scalar.activation(win_abs[j][:, :N], b_ps[j][:], ACT.Abs)
             if j == 0:
-                nc.scalar.activation(win_num[j][:, N:], b_ps[j][:], ACT.Abs)
+                nc.scalar.activation(win_d[j][:, N:], b_ps[j][:], ACT.Abs)
             else:
-                nc.sync.dma_start(win_num[j][:, N:], win_abs[j][:, :N])
+                nc.sync.dma_start(win_d[j][:, N:], win_abs[j][:, :N])
         d_ps = project(1, 4)
         for j in range(J):
             nc.scalar.copy(win_d[j][:, :N], d_ps[j][:])
@@ -152,25 +150,29 @@ def tile_picked_twkjointbnorm2hopp_none_po_kernel(
         pick_scales(0)
         y_ps = project(0, 0)
 
+        den_late = sb("den_late", [P, 2, N], F32)
+        den = (win_num[0][:, N:], win_num[1][:, N:], den_late[:, 0, :], den_late[:, 1, :])
         for j in range(J):
-            nc.vector.tensor_tensor(win_d[j][:, N:], win_abs[j][:].indirect(l_n4[:]), win_num[j][:, N:], ALU.add)
+            nc.vector.tensor_tensor(den[j], win_abs[j][:].indirect(l_n4[:]), win_d[j][:, N:], ALU.add)
         lnden = sb("lnden", [P, J, N], F32)
+        for j in range(2):
+            nc.scalar.activation(lnden[:, j, :], den[j], ACT.Ln, bias=half[:])
+        nc.scalar.activation(lnden[:, 2:, :], den_late[:], ACT.Ln, bias=half[:])
+        rec = (den_late[:, 0, :], den_late[:, 1, :], win_num[3][:, N:], win_num[2][:, N:])
         for j in range(J):
-            nc.scalar.activation(lnden[:, j, :], win_d[j][:, N:], ACT.Ln, bias=half[:])
-        rec = sb("rec", [P, J, N], F32)
-        for j in range(J):
-            nc.scalar.activation(rec[:, j, :], lnden[:, j, :], ACT.Exp, scale=-1.0)
+            nc.scalar.activation(rec[j], lnden[:, j, :], ACT.Exp, scale=-1.0)
 
-        d2 = sb("d2", [P, J, N], F32)
+        d2_last = sb("d2_last", [P, N], F32)
+        d2 = (win_abs[3][:, :N], win_abs[3][:, N:], win_d[3][:, N:], d2_last[:])
         for j in range(J):
-            nc.vector.tensor_copy(d2[:, j, :], win_d[j][:].indirect(l_n2[:]))
+            nc.vector.tensor_copy(d2[j], win_d[j][:].indirect(l_n2[:]))
         th = sb("th", [P, J, N], F32)
         yg = lnden
         z2f = sb("z2f", [P, J, N], F32)
 
         def difference(j):
-            diff = rec[:, j, :]
-            nc.vector.tensor_tensor(diff, win_d[j][:].indirect(l_n1[:]), d2[:, j, :], ALU.subtract)
+            diff = (rec[3], win_num[3][:, :N], win_num[3][:, N:], d2[0])[j]
+            nc.vector.tensor_tensor(diff, win_d[j][:].indirect(l_n1[:]), d2[j], ALU.subtract)
             nc.scalar.activation(
                 th[:, j, :].rearrange("p (u m) -> p m u", u=J),
                 diff.rearrange("p (m u) -> p m u", u=J),
@@ -178,7 +180,7 @@ def tile_picked_twkjointbnorm2hopp_none_po_kernel(
             )
 
         for j in range(J):
-            nc.vector.tensor_tensor(z2f[:, j, :], win_num[j][:].indirect(l_n3[:]), rec[:, j, :], ALU.mult)
+            nc.vector.tensor_tensor(z2f[:, j, :], win_num[j][:].indirect(l_n3[:]), rec[j], ALU.mult)
         for j in range(J):
             nc.scalar.activation(
                 yg[:, j, :].rearrange("p (u m) -> p u m", u=J),
@@ -255,8 +257,7 @@ def tile_picked_twkjointbnorm2hopp_none_po_kernel(
                     res[c][:, u, :], win_num[u][:].indirect(l_n6[:, lo // 16 : hi // 16]), st[:, u, lo:hi], ALU.mult
                 )
             nc.sync.dma_start(out_rows[:, :, lo:hi], res[c][:])
-            engine_copy = nc.scalar.copy if c + 1 < len(chunks) else nc.vector.tensor_copy
-            engine_copy(
+            nc.scalar.copy(
                 resb[c][:].rearrange("p (c i u) -> p c u i", i=4, u=J),
                 res[c][:].rearrange("p u (c i) -> p c u i", i=4),
             )

@@ -87,11 +87,6 @@ def tile_picked_twkjointbnorm2hopp_none_po_kernel(
         load_weight(1)
         l_n4 = load_list("l_n4", n4)
         load_weight(0)
-        l_n2 = load_list("l_n2", n2)
-        l_n1 = load_list("l_n1", n1)
-        l_n3 = load_list("l_n3", n3)
-        l_n5 = load_list("l_n5", n5)
-        l_n6 = load_list("l_n6", n6)
 
         gain_ps = bank(7, "gain_ps")
         nc.tensor.transpose(gain_ps[:, :P], gain_rows[:], ident[:])
@@ -138,10 +133,12 @@ def tile_picked_twkjointbnorm2hopp_none_po_kernel(
         b_ps = project(2, 0)
         for j in range(J):
             nc.scalar.activation(win_abs[j][:, :N], b_ps[j][:], ACT.Abs)
-            if j == 0:
-                nc.scalar.activation(win_d[j][:, N:], b_ps[j][:], ACT.Abs)
-            else:
-                nc.sync.dma_start(win_d[j][:, N:], win_abs[j][:, :N])
+            nc.sync.dma_start(win_d[j][:, N:], win_abs[j][:, :N])
+        l_n2 = load_list("l_n2", n2)
+        l_n1 = load_list("l_n1", n1)
+        l_n3 = load_list("l_n3", n3)
+        l_n5 = load_list("l_n5", n5)
+        l_n6 = load_list("l_n6", n6)
         d_ps = project(1, 4)
         for j in range(J):
             nc.scalar.copy(win_d[j][:, :N], d_ps[j][:])

@@ -87,6 +87,11 @@ def tile_picked_twkjointbnorm2hopp_none_po_kernel(
         load_weight(1)
         l_n4 = load_list("l_n4", n4)
         load_weight(0)
+        l_n2 = load_list("l_n2", n2)
+        l_n1 = load_list("l_n1", n1)
+        l_n3 = load_list("l_n3", n3)
+        l_n5 = load_list("l_n5", n5)
+        l_n6 = load_list("l_n6", n6)
 
         gain_ps = bank(7, "gain_ps")
         nc.tensor.transpose(gain_ps[:, :P], gain_rows[:], ident[:])
@@ -104,7 +109,7 @@ def tile_picked_twkjointbnorm2hopp_none_po_kernel(
         pick_scales(2)
         pick_scales(1)
 
-        def project(a, first_bank):
+        def pick_words(a):
             nc.vector.tensor_copy(
                 ww[a][:].bitcast(I32).rearrange("p (j g w) -> p j g w", j=J, w=4),
                 ww_raw[a][:].bitcast(I32).rearrange("p (g j w) -> p j g w", j=J, w=4),
@@ -115,9 +120,12 @@ def tile_picked_twkjointbnorm2hopp_none_po_kernel(
             )
             xw_g = sb("xw_g%d" % a, [P, N], I32, tag="ws_raw%d" % a)
             nc.vector.tensor_copy(xw_g[:].bitcast(U32), xw[:].bitcast(U32).indirect(lists[a][:]))
+            return xw_g
+
+        def project(a, xw_g, bank_of):
             banks = []
             for j in range(J):
-                acc = bank(first_bank + j, "proj%d_%d" % (a, j))
+                acc = bank(bank_of[j], "proj%d_%d" % (a, j))
                 nc.tensor.matmul_mx(
                     acc[:],
                     lhsT=ww[a][:, 2 * P * j : 2 * P * (j + 1)].bitcast(FP4X4),
@@ -130,41 +138,46 @@ def tile_picked_twkjointbnorm2hopp_none_po_kernel(
                 banks.append(acc)
             return banks
 
-        b_ps = project(2, 0)
+        b_ps = project(2, pick_words(2), (0, 1, 2, 3))
         for j in range(J):
             nc.scalar.activation(win_abs[j][:, :N], b_ps[j][:], ACT.Abs)
-            nc.sync.dma_start(win_d[j][:, N:], win_abs[j][:, :N])
-        l_n2 = load_list("l_n2", n2)
-        l_n1 = load_list("l_n1", n1)
-        l_n3 = load_list("l_n3", n3)
-        l_n5 = load_list("l_n5", n5)
-        l_n6 = load_list("l_n6", n6)
-        d_ps = project(1, 4)
+        d_ps = project(1, pick_words(1), (4, 5, 6, 7))
         for j in range(J):
             nc.scalar.copy(win_d[j][:, :N], d_ps[j][:])
         for j in range(J):
             nc.scalar.activation(win_num[j][:, :N], b_ps[j][:], ACT.Copy, scale=gains[:, J + j : J + j + 1])
         pick_scales(0)
-        y_ps = project(0, 0)
 
-        den_late = sb("den_late", [P, 2, N], F32)
-        den = (win_num[0][:, N:], win_num[1][:, N:], den_late[:, 0, :], den_late[:, 1, :])
+        blocks = [slice(P * c, P * (c + 1)) for c in range(J)]
+        spare = sb("spare", [P, 2 * N], F32)
+        ln_early = sb("ln_early", [P, J - 1, N], F32)
+        ln_t = (ln_early[:, 0, :], ln_early[:, 1, :], ln_early[:, 2, :], spare[:, N // 2 : N // 2 + N])
         for j in range(J):
-            nc.vector.tensor_tensor(den[j], win_abs[j][:].indirect(l_n4[:]), win_d[j][:, N:], ALU.add)
-        lnden = sb("lnden", [P, J, N], F32)
-        for j in range(2):
-            nc.scalar.activation(lnden[:, j, :], den[j], ACT.Ln, bias=half[:])
-        nc.scalar.activation(lnden[:, 2:, :], den_late[:], ACT.Ln, bias=half[:])
-        rec = (den_late[:, 0, :], den_late[:, 1, :], win_num[3][:, N:], win_num[2][:, N:])
+            nc.vector.tensor_copy(win_d[j][:, N:], win_abs[j][:].indirect(l_n4[:]))
+            den_t = bank(4 + j, "den_t%d" % j)
+            for c in blocks:
+                nc.tensor.matmul(den_t[:, c], lhsT=win_abs[j][:, :N][:, c], rhs=ident[:], is_transpose=True, start=True, stop=False)
+                nc.tensor.matmul(den_t[:, c], lhsT=win_d[j][:, N:][:, c], rhs=ident[:], is_transpose=True, start=False, stop=True)
+            nc.scalar.activation(ln_t[j], den_t[:], ACT.Ln, bias=half[:])
+        y_words = pick_words(0)
+        rec = (spare[:, :N], spare[:, N:], win_num[3][:, N:], win_num[2][:, N:])
+        back_bank = (4, 5, 7, 6)
+        ln_ps = []
         for j in range(J):
-            nc.scalar.activation(rec[j], lnden[:, j, :], ACT.Exp, scale=-1.0)
+            ln_den = bank(back_bank[j], "ln_den%d" % j)
+            for c in blocks:
+                nc.tensor.transpose(ln_den[:, c], ln_t[j][:, c], ident[:])
+            ln_ps.append(ln_den)
+        for j in range(J):
+            nc.scalar.activation(rec[j], ln_ps[j][:], ACT.Exp, scale=-1.0)
+        y_ps = project(0, y_words, back_bank)
 
-        d2_last = sb("d2_last", [P, N], F32)
-        d2 = (win_abs[3][:, :N], win_abs[3][:, N:], win_d[3][:, N:], d2_last[:])
+        d2_tile = sb("d2_tile", [P, J, N], F32)
+        d2 = [d2_tile[:, j, :] for j in range(J)]
         for j in range(J):
             nc.vector.tensor_copy(d2[j], win_d[j][:].indirect(l_n2[:]))
         th = sb("th", [P, J, N], F32)
-        yg = lnden
+        yg = sb("yg", [P, J, N], F32)
         z2f = sb("z2f", [P, J, N], F32)
 
         def difference(j):
@@ -211,7 +224,7 @@ def tile_picked_twkjointbnorm2hopp_none_po_kernel(
 
         def scores(u):
             nc.vector.quantize_mx(out=zw[u][:].bitcast(FP8X4), scales=zs[u][:], in_=zb[u][:])
-            acc = bank(4 + u, "s_ps%d" % u)
+            acc = bank(u, "s_ps%d" % u)
             nc.tensor.matmul_mx(
                 acc[:],
                 lhsT=zw[u][:].bitcast(FP8X4),

from contextlib import ExitStack

import concourse.mybir as mybir
from concourse.masks import make_identity

F32 = mybir.dt.float32
BF16 = mybir.dt.bfloat16
I32 = mybir.dt.int32
U32 = mybir.dt.uint32
U16 = mybir.dt.uint16
U8 = mybir.dt.uint8
FP8X4 = mybir.dt.float8_e4m3fn_x4
FP4X4 = mybir.dt.float4_e2m1fn_x4
ALU = mybir.AluOpType
ACT = mybir.ActivationFunctionType

P = 128
T = 2048
N = 512
J = 4

FLOPS = 4 * 2 * 512 * 512 * 512


def tile_picked_twkjointbnorm2hopp_none_po_kernel(
    tc, x_words, x_scales, w1_words, w1_scales, w2_words, w2_scales, w3_words, w3_scales,
    ga, gb, offs, two, n1, n2, three, n3, n4, n5, n6, out_0, out_1, out_2,
):
    nc = tc.nc
    with ExitStack() as ctx:
        keep = ctx.enter_context(tc.tile_pool(name="keep", bufs=1))
        psum = ctx.enter_context(tc.psum_pool(name="psum", bufs=1))

        def sb(name, shape, dtype, tag=None):
            return keep.tile(shape, dtype, name=name, tag=tag or name, align_bytes=64)

        def bank(k, name):
            return psum.tile([P, N], F32, name=name, tag="bank%d" % k)

        def load_list(name, src):
            tile = sb(name, [P, N // 16], U16)
            nc.sync.dma_start(tile[:], src)
            return tile

        def load_scale_rows(queue, tile, src):
            for q in range(4):
                queue.dma_start(tile[32 * q : 32 * q + 4, :].bitcast(I32), src[0, 4 * q : 4 * q + 4, :].bitcast(I32))

        xs = sb("xs", [P, T], U8)
        nc.gpsimd.memset(xs[:].bitcast(I32), 0)
        ws_raw = [sb("ws_raw%d" % a, [P, N], U8) for a in range(3)]
        for a in (2, 1, 0):
            nc.vector.memset(ws_raw[a][:].bitcast(I32), 0)
        win_abs = [sb("win_abs%d" % j, [P, 2 * N], F32) for j in range(J)]
        win_num = [sb("win_num%d" % j, [P, 2 * N], F32) for j in range(J)]
        win_d = [sb("win_d%d" % j, [P, 2 * N], F32) for j in range(J)]

        half = sb("half", [P, 1], F32)
        nc.gpsimd.memset(half[:], 0.5)
        warm = sb("warm", [P, 1], F32)
        nc.scalar.activation(warm[:], half[:], ACT.Ln)
        gain_rows = sb("gain_rows", [P, P], F32)
        nc.gpsimd.memset(gain_rows[:], 0.0)
        for r, gain in enumerate((ga, gb)):
            nc.gpsimd.dma_start(
                gain_rows[J * r : J * r + J, :].rearrange("j (g i) -> j g i", i=8),
                gain.rearrange("(g j i) o -> j g (i o)", j=J, i=8),
            )
        ident = sb("ident", [P, P], F32)
        make_identity(nc, ident[:])

        l_three = load_list("l_three", three)
        load_scale_rows(nc.sync, xs, x_scales)
        l_two = load_list("l_two", two)
        xw = sb("xw", [P, T], I32)
        nc.sync.dma_start(xw[:], x_words[0].rearrange("p n t -> p (n t)").bitcast(I32))
        ww_raw = [sb("ww_raw%d" % a, [P, 2 * N], U8) for a in range(3)]
        w_words = (w1_words, w2_words, w3_words)
        w_scales = (w1_scales, w2_scales, w3_scales)

        def load_weight(a):
            nc.sync.dma_start(ww_raw[a][:].bitcast(I32), w_words[a][0].bitcast(I32))
            load_scale_rows(nc.sync, ws_raw[a], w_scales[a])

        load_weight(2)
        l_offs = load_list("l_offs", offs)
        load_weight(1)
        l_n4 = load_list("l_n4", n4)
        load_weight(0)
        l_n2 = load_list("l_n2", n2)
        l_n1 = load_list("l_n1", n1)
        l_n3 = load_list("l_n3", n3)
        l_n5 = load_list("l_n5", n5)
        l_n6 = load_list("l_n6", n6)

        gain_ps = bank(7, "gain_ps")
        nc.tensor.transpose(gain_ps[:, :P], gain_rows[:], ident[:])
        gains = sb("gains", [P, 2 * J], F32)
        nc.scalar.copy(gains[:], gain_ps[:, : 2 * J])

        lists = (l_offs, l_two, l_three)
        xs_g = [sb("xs_g%d" % a, [P, N], U8) for a in range(3)]
        ww = [sb("ww%d" % a, [P, 2 * N], U8) for a in range(3)]
        ws = [sb("ws%d" % a, [P, N], U8) for a in range(3)]

        def pick_scales(a):
            nc.vector.tensor_copy(xs_g[a][:], xs[:].indirect(lists[a][:]))

        pick_scales(2)
        pick_scales(1)

        def pick_words(a):
            nc.vector.tensor_copy(
                ww[a][:].bitcast(I32).rearrange("p (j g w) -> p j g w", j=J, w=4),
                ww_raw[a][:].bitcast(I32).rearrange("p (g j w) -> p j g w", j=J, w=4),
            )
            nc.vector.tensor_copy(
                ws[a][:].bitcast(I32).rearrange("p (j g w) -> p j g w", j=J, w=2),
                ws_raw[a][:].bitcast(I32).rearrange("p (g j w) -> p j g w", j=J, w=2),
            )
            xw_g = sb("xw_g%d" % a, [P, N], I32, tag="ws_raw%d" % a)
            nc.vector.tensor_copy(xw_g[:].bitcast(U32), xw[:].bitcast(U32).indirect(lists[a][:]))
            return xw_g

        def project(a, xw_g, bank_of):
            banks = []
            for j in range(J):
                acc = bank(bank_of[j], "proj%d_%d" % (a, j))
                nc.tensor.matmul_mx(
                    acc[:],
                    lhsT=ww[a][:, 2 * P * j : 2 * P * (j + 1)].bitcast(FP4X4),
                    lhsT_scale=ws[a][:, P * j : P * (j + 1)],
                    rhs=xw_g[:].bitcast(FP8X4),
                    rhs_scale=xs_g[a][:],
                    start=True,
                    stop=True,
                )
                banks.append(acc)
            return banks

        b_ps = project(2, pick_words(2), (0, 1, 2, 3))
        for j in range(J):
            nc.scalar.activation(win_abs[j][:, :N], b_ps[j][:], ACT.Abs)
        d_ps = project(1, pick_words(1), (4, 5, 6, 7))
        for j in range(J):
            nc.scalar.copy(win_d[j][:, :N], d_ps[j][:])
        for j in range(J):
            nc.scalar.activation(win_num[j][:, :N], b_ps[j][:], ACT.Copy, scale=gains[:, J + j : J + j + 1])
        pick_scales(0)

        blocks = [slice(P * c, P * (c + 1)) for c in range(J)]
        spare = sb("spare", [P, 2 * N], F32)
        ln_early = sb("ln_early", [P, J - 1, N], F32)
        ln_t = (ln_early[:, 0, :], ln_early[:, 1, :], ln_early[:, 2, :], spare[:, N // 2 : N // 2 + N])
        for j in range(J):
            nc.vector.tensor_copy(win_d[j][:, N:], win_abs[j][:].indirect(l_n4[:]))
            den_t = bank(4 + j, "den_t%d" % j)
            for c in blocks:
                nc.tensor.matmul(den_t[:, c], lhsT=win_abs[j][:, :N][:, c], rhs=ident[:], is_transpose=True, start=True, stop=False)
                nc.tensor.matmul(den_t[:, c], lhsT=win_d[j][:, N:][:, c], rhs=ident[:], is_transpose=True, start=False, stop=True)
            nc.scalar.activation(ln_t[j], den_t[:], ACT.Ln, bias=half[:])
        y_words = pick_words(0)
        rec = (spare[:, :N], spare[:, N:], win_num[3][:, N:], win_num[2][:, N:])
        back_bank = (4, 5, 7, 6)
        ln_ps = []
        for j in range(J):
            ln_den = bank(back_bank[j], "ln_den%d" % j)
            for c in blocks:
                nc.tensor.transpose(ln_den[:, c], ln_t[j][:, c], ident[:])
            ln_ps.append(ln_den)
        for j in range(J):
            nc.scalar.activation(rec[j], ln_ps[j][:], ACT.Exp, scale=-1.0)
        y_ps = project(0, y_words, back_bank)

        d2_tile = sb("d2_tile", [P, J, N], F32)
        d2 = [d2_tile[:, j, :] for j in range(J)]
        for j in range(J):
            nc.vector.tensor_copy(d2[j], win_d[j][:].indirect(l_n2[:]))
        th = sb("th", [P, J, N], F32)
        yg = sb("yg", [P, J, N], F32)
        z2f = sb("z2f", [P, J, N], F32)

        def difference(j):
            diff = (rec[3], win_num[3][:, :N], win_num[3][:, N:], d2[0])[j]
            nc.vector.tensor_tensor(diff, win_d[j][:].indirect(l_n1[:]), d2[j], ALU.subtract)
            nc.scalar.activation(
                th[:, j, :].rearrange("p (u m) -> p m u", u=J),
                diff.rearrange("p (m u) -> p m u", u=J),
                ACT.Tanh,
            )

        for j in range(J):
            nc.vector.tensor_tensor(z2f[:, j, :], win_num[j][:].indirect(l_n3[:]), rec[j], ALU.mult)
        for j in range(J):
            nc.scalar.activation(
                yg[:, j, :].rearrange("p (u m) -> p u m", u=J),
                y_ps[j][:].rearrange("p (m u) -> p u m", u=J),
                ACT.Copy,
                scale=gains[:, j : j + 1],
            )
        z2b = sb("z2b", [P, J * N], BF16)
        nc.scalar.copy(
            z2b[:].rearrange("p (c i j) -> p c j i", i=4, j=J),
            z2f[:].rearrange("p j (c i) -> p c j i", i=4),
        )
        for j in range(J):
            difference(j)
        z2w = sb("z2w", [P, N], U32)
        z2s = sb("z2s", [P, N], U8)
        nc.vector.quantize_mx(out=z2w[:].bitcast(FP8X4), scales=z2s[:], in_=z2b[:])

        zb = [sb("zb%d" % u, [P, J * P], BF16) for u in range(J)]
        zw = [sb("zw%d" % u, [P, P], U32) for u in range(J)]
        zs = [sb("zs%d" % u, [P, P], U8) for u in range(J)]

        def make_z(u):
            cols = slice(P * u, P * (u + 1))
            nc.vector.tensor_tensor(
                zb[u][:].rearrange("p (c i j) -> p c j i", i=4, j=J),
                yg[:, :, cols].rearrange("p j (c i) -> p c j i", i=4),
                th[:, :, cols].rearrange("p j (c i) -> p c j i", i=4),
                ALU.mult,
            )

        def scores(u):
            nc.vector.quantize_mx(out=zw[u][:].bitcast(FP8X4), scales=zs[u][:], in_=zb[u][:])
            acc = bank(u, "s_ps%d" % u)
            nc.tensor.matmul_mx(
                acc[:],
                lhsT=zw[u][:].bitcast(FP8X4),
                lhsT_scale=zs[u][:],
                rhs=z2w[:].bitcast(FP8X4),
                rhs_scale=z2s[:],
                start=True,
                stop=True,
            )
            nc.scalar.activation(win_abs[u][:, :N], acc[:], ACT.Copy, scale=0.0625)
            nc.scalar.activation(win_num[u][:, N:], acc[:], ACT.Copy, scale=0.0625)

        make_z(0)
        for u in range(J):
            if u + 1 < J:
                make_z(u + 1)
            scores(u)

        st = sb("st", [P, J, N], F32)
        for u in range(J):
            nc.vector.tensor_tensor(st[:, u, :], win_abs[u][:].indirect(l_n5[:]), win_num[u][:, N:], ALU.add)
            nc.scalar.activation(win_num[u][:, :N], st[:, u, :], ACT.Tanh)

        out_rows = out_0.rearrange("(p u) v -> p u v", u=J)
        words_out = out_1[0].rearrange("p n t -> p (n t)").bitcast(I32)
        ow = sb("ow", [P, N], I32)
        osc = sb("osc", [P, N], U8)
        chunks = ((0, 256), (256, 384), (384, 512))
        res = [sb("res%d" % c, [P, J, hi - lo], F32) for c, (lo, hi) in enumerate(chunks)]
        resb = [sb("resb%d" % c, [P, J * (hi - lo)], BF16) for c, (lo, hi) in enumerate(chunks)]

        def quantise_out(c):
            lo, hi = chunks[c]
            nc.vector.quantize_mx(out=ow[:, lo:hi].bitcast(FP8X4), scales=osc[:, lo:hi], in_=resb[c][:])
            nc.sync.dma_start(words_out[:, lo:hi], ow[:, lo:hi])

        for c, (lo, hi) in enumerate(chunks):
            for u in range(J):
                nc.vector.tensor_tensor(
                    res[c][:, u, :], win_num[u][:].indirect(l_n6[:, lo // 16 : hi // 16]), st[:, u, lo:hi], ALU.mult
                )
            nc.sync.dma_start(out_rows[:, :, lo:hi], res[c][:])
            nc.scalar.copy(
                resb[c][:].rearrange("p (c i u) -> p c u i", i=4, u=J),
                res[c][:].rearrange("p u (c i) -> p c u i", i=4),
            )
        for c in range(len(chunks)):
            quantise_out(c)
        for q in range(4):
            queue = nc.scalar if q % 2 else nc.sync
            queue.dma_start(out_2[0, 4 * q : 4 * q + 4, :].bitcast(I32), osc[32 * q : 32 * q + 4, :].bitcast(I32))
